import numpy as np, ml_dtypes
CORES = [8,80,112,136,208,240,264,336,368,392,464,496]
N = 12
R, NS, T = 4096, 1024, 32
def entries(a): return a.T.reshape(-1)
def pack(v, P): return np.ascontiguousarray(np.asarray(v, np.int32).reshape(-1, P).T)
def lists(rng, how):
    I = rng.integers(0, N * R, NS)
    if how == "alike": I[:] = rng.integers(N * R)
    if how == "distinct": I = rng.permutation(N * R)[:NS]
    if how == "hotrank": I = R * int(rng.integers(N)) + rng.integers(0, R, NS)
    if how == "edge": I = R * rng.integers(0, N, NS) + np.where(rng.random(NS) < 0.5, 0, R - 1)
    if how == "sorted": I = np.sort(I)
    return {"neg": np.broadcast_to(pack(I, 16), (N, 16, NS // 16)).copy()}
def setup_inputs(rng):
    return dict({"h": rng.standard_normal((N, 128, T), dtype=np.float32).astype(ml_dtypes.bfloat16), "tab": (rng.standard_normal((N, 128, R), dtype=np.float32) / 8).astype(ml_dtypes.bfloat16)}, **lists(rng, "uniform"))
def setup_inputs_alike(rng):
    d = setup_inputs(rng); d.update(lists(rng, "alike"))
    for k in ("h", "tab"): d[k] = (d[k].astype(np.float32) * 1024.0).astype(d[k].dtype)
    return d
def setup_inputs_distinct(rng):
    d = setup_inputs(rng); d.update(lists(rng, "distinct"))
    for k in ("h", "tab"): d[k] = (d[k].astype(np.float32) * (1 / 1024.0)).astype(d[k].dtype)
    return d
def setup_inputs_edge(rng):
    d = setup_inputs(rng); d.update(lists(rng, "edge"))
    return d
def setup_inputs_hotrank(rng):
    d = setup_inputs(rng); d.update(lists(rng, "hotrank"))
    return d
def setup_inputs_sorted(rng):
    d = setup_inputs(rng); d.update(lists(rng, "sorted"))
    return d
def check_inputs(x):
    bad = []
    if x["neg"].min() < 0 or x["neg"].max() >= N * R: bad.append("neg out of range")
    if not all(np.array_equal(a, x["neg"][0]) for a in x["neg"]): bad.append("neg isn't alike on all ranks")
    return bad
def reference(h, tab, neg):
    A = np.concatenate(list(tab), axis=1).astype(np.float64)
    S = A[:, entries(neg[0])]
    return {"y": np.stack([h[r].astype(np.float64).T @ S for r in range(N)]).astype(ml_dtypes.bfloat16)}

@@ -1,0 +1,255 @@
+from concourse.bass import DstId, RemoteDMATransfer
+from concourse.mybir import AluOpType, ActivationFunctionType
+
+NSIM = 512
+R, NS, TOK = 4096, 1024, 32
+PAD = 8
+LANES, LW, BW = 4, 256, 128
+SERVED = 6
+
+SCRATCH = {
+    "win": ("sbuf", [128, PAD + R + PAD], "bfloat16"),
+    "negs": ("sbuf", [128, NS // 16], "int32"),
+    "offi": ("sbuf", [128, NS // 16], "int32"),
+    "off": ("sbuf", [128, NS // 16], "uint16"),
+    "hsb": ("sbuf", [128, TOK], "bfloat16"),
+    "S": ("sbuf", [128, NS], "bfloat16"),
+    "ident": ("sbuf", [128, 128], "bfloat16"),
+    "land": ("sbuf", [128, SERVED * LANES * 2 * TOK], "bfloat16"),
+    "ysb": ("sbuf", [128, 256], "bfloat16"),
+    "sown": ("sbuf", [128, LW], "bfloat16"),
+    "sfar": ("sbuf", [128, LW], "bfloat16"),
+    "Hd": ("sbuf", [128, SERVED * TOK], "bfloat16"),
+    "osb": ("sbuf", [128, SERVED, 2, TOK], "bfloat16"),
+    "ps0": ("psum", [128, 512], "float32"),
+    "ps1": ("psum", [128, 512], "float32"),
+}
+SEMAPHORES = ["hld", "negld", "tabld", "vz", "of1", "of2", "gA", "gB", "idn", "hown", "hpeer", "sowns", "sfars",
+              "mm0", "mm1", "cp", "pd0", "pd1", "ycp", "st", "lsem"] + ["y%d_%d" % (i, L) for i in range(SERVED) for L in range(2)]
+
+_C = {}
+
+
+def _engines(m):
+    return [e for e in range(16) if (m >> e) & 1]
+
+
+def _bits(es):
+    return sum(1 << e for e in es)
+
+
+def _plan(T, topo):
+    if "p" in _C:
+        return _C["p"]
+    cores = list(T.cores)
+    n = len(cores)
+    hosts = sorted({topo.host(c) for c in cores})
+    byhost = {H: [q for q in range(n) if topo.host(cores[q]) == H] for H in hosts}
+
+    def twin(q, G):
+        return [p for p in byhost[G] if topo.chip(cores[p]) == topo.chip(cores[q])][0]
+
+    near, far = {}, {}
+    for H in hosts:
+        a = byhost[H][0]
+        for G in hosts:
+            if G != H and topo.may_write(cores[a], cores[twin(a, G)]):
+                if topo.rack(G) == topo.rack(H):
+                    near[H] = G
+                else:
+                    far[H] = G
+    owners = []
+    for q in range(n):
+        c = cores[q]
+        H = topo.host(c)
+        reach = [cores[p] for G in (H, near[H], far[H]) for p in byhost[G]]
+        owners.append([w for w in range(NSIM) if w != c and topo.host(w) == H and topo.chip(w) == topo.chip(c)
+                       and all(topo.may_write(w, d) for d in reach)][:LANES])
+    kind, seen = [], {}
+    for w in owners[0]:
+        k = seen.get(topo.die(w), 0)
+        kind.append(k % 2)
+        seen[topo.die(w)] = k + 1
+
+    def fold(H, l):
+        return near[H] if kind[l] == 0 else far[H]
+
+    def serve(H, l):
+        return far[H] if kind[l] == 0 else near[H]
+
+    def served(H, l):
+        return byhost[H] + byhost[serve(H, l)]
+
+    def targets(q, l):
+        H = topo.host(cores[q])
+        D = served(H, l)
+        return [p for p in D if topo.host(cores[p]) != H] + [p for p in D if topo.host(cores[p]) == H and p != q]
+
+    def off_engines(q, l):
+        m = topo.mask(owners[q][l], cores[q])
+        for p in targets(q, l):
+            m &= topo.mask(owners[q][l], cores[p]) & topo.mask(owners[q][l], owners[p][l])
+        return _engines(m)
+
+    def hplan(q, l):
+        t, es = targets(q, l), off_engines(q, l)
+        k = len(es) // 4
+        return [[(t[j], es[k * j:k * j + k]) for j in range(4)], [(t[4], es)]]
+
+    def yplan(q, l):
+        t, es = targets(q, l), off_engines(q, l)
+        k, h = len(es) // 4, len(es) // 2
+        return [[(t[j], es[k * j:k * j + k]) for j in range(4)], [(t[4], es[:h]), (q, es[h:])]]
+
+    def count(plan, src, l, dst):
+        return sum(len(e) for call in plan(src, l) for (p, e) in call if p == dst)
+
+    P = {"cores": cores, "owners": owners, "twin": twin, "fold": fold, "served": served, "hplan": hplan, "yplan": yplan,
+         "count": count, "relay": {owners[q][l]: (q, l) for q in range(n) for l in range(LANES)}}
+    _C["p"] = P
+    return P
+
+
+def _tr(topo, src_core, dst_core, es, sem, src, dst):
+    rid, pid = topo.addr(dst_core, src_core)
+    return RemoteDMATransfer(dst_ids=[DstId(rid=rid, pnc=pid)], dma_engine_mask=_bits(es), remote_sem=sem, src=src, dst=dst)
+
+
+def _rank(g, core, r, T, topo, P):
+    s = T.sem
+    cores, owners = P["cores"], P["owners"]
+    H = topo.host(core)
+    v, sc, sy, pe = g.vector, g.scalar, g.sync, g.tensor
+
+    sy.dma_start(T.hsb[:], T.h[:]).then_inc(s.hld, 16)
+    for q in range(8):
+        (sy if q < 4 else sc).dma_start(T.negs[16 * q:16 * q + 16, :], T.neg[:]).then_inc(s.negld, 16)
+    sy.dma_start(T.win[0:64, PAD:PAD + R], T.tab[0:64, :]).then_inc(s.tabld, 16)
+    sc.dma_start(T.win[64:128, PAD:PAD + R], T.tab[64:128, :]).then_inc(s.tabld, 16)
+
+    v.memset(T.win[:, 0:PAD], 0.0).then_inc(s.vz, 1)
+    v.memset(T.win[:, PAD + R:PAD + R + PAD], 0.0).then_inc(s.vz, 1)
+    v.memset(T.ident[:], 1.0).then_inc(s.vz, 1)
+    v.wait_ge(s.negld, 128)
+    v.tensor_scalar(out=T.offi[:], in0=T.negs[:], scalar1=float(PAD - R * r), scalar2=0.0,
+                    op0=AluOpType.add, op1=AluOpType.max).then_inc(s.of1, 1)
+    v.wait_ge(s.of1, 1)
+    v.tensor_scalar(out=T.off[:], in0=T.offi[:], scalar1=float(PAD + R), scalar2=None, op0=AluOpType.min).then_inc(s.of2, 1)
+
+    g.wait_ge(s.hld, 16)
+    on = _engines(topo.mask(core, owners[r][0]))
+    k = len(on) // LANES
+    g.remote_dma_fused([_tr(topo, core, owners[r][l], on[k * l:k * l + k], s.hown, T.hsb[:],
+                            T.Hd[:, TOK * P["served"](H, l).index(r):TOK * P["served"](H, l).index(r) + TOK])
+                        for l in range(LANES)], local_sem=s.lsem)
+    lsum = len(on)
+    g.wait_ge(s.vz, 3)
+    g.affine_select(out=T.ident[:], in_=T.ident[:], pattern=[[-1, 128]], compare_op=AluOpType.is_equal, fill=0.0,
+                    base=0, channel_multiplier=1).then_inc(s.idn, 1)
+
+    for q in (v, sc):
+        q.wait_ge(s.of2, 1)
+        q.wait_ge(s.vz, 3)
+        q.wait_ge(s.tabld, 32)
+    for l in range(LANES):
+        L, bh = l // 2, l % 2
+        for x in range(2):
+            m = 2 * (2 * bh + x) + L
+            out = T.S[:, (2 * l + x) * BW:(2 * l + x + 1) * BW]
+            src = T.win[:, 0:PAD + R + PAD].indirect(T.off[:, 8 * m:8 * m + 8])
+            if bh == 0:
+                v.tensor_copy(out=out, in_=src).then_inc(s.gA if L == 0 else s.gB, 1)
+            else:
+                sc.activation(out=out, in_=src, func=ActivationFunctionType.Copy).then_inc(s.gA if L == 0 else s.gB, 1)
+    for L in range(2):
+        g.wait_ge(s.gA if L == 0 else s.gB, 4)
+        trs = []
+        for j, l in enumerate((2 * L, 2 * L + 1)):
+            dfar = owners[P["twin"](r, P["fold"](H, l))][l]
+            offc = _engines(topo.mask(core, dfar))
+            onl = [e for e in on if e not in offc]
+            h1, h2 = len(onl) // 2, len(offc) // 2
+            blk = T.S[:, l * LW:(l + 1) * LW]
+            trs.append(_tr(topo, core, owners[r][l], onl[h1 * j:h1 * j + h1], s.sowns, blk, T.sown[:]))
+            trs.append(_tr(topo, core, dfar, offc[h2 * j:h2 * j + h2], s.sfars, blk, T.sfar[:]))
+            lsum += h1 + h2
+        g.remote_dma_fused(trs, local_sem=s.lsem)
+
+    pe.wait_ge(s.idn, 1)
+    for L in range(2):
+        ps = T.ps0 if L == 0 else T.ps1
+        for i in range(SERVED):
+            cnt = sum(P["count"](P["yplan"], P["served"](H, l)[i], l, r) for l in (2 * L, 2 * L + 1))
+            pe.wait_ge(s["y%d_%d" % (i, L)], cnt)
+            a = (i * LANES + 2 * L) * 2 * TOK
+            mm = pe.matmul(ps[:, 0:128], T.land[:, a:a + 128], T.ident[:], start=(i == 0), stop=(i == SERVED - 1))
+        mm.then_inc(s.pd0 if L == 0 else s.pd1, 1)
+        v.wait_ge(s.pd0 if L == 0 else s.pd1, 1)
+        v.tensor_copy(out=T.ysb[:, 128 * L:128 * L + 128], in_=ps[:, 0:128]).then_inc(s.ycp, 1)
+    for b in range(4):
+        q = sy if b < 2 else sc
+        if b % 2 == 0:
+            q.wait_ge(s.ycp, 2)
+        q.dma_start(T.y[:, 256 * b:256 * b + 256], T.ysb[32 * b:32 * b + 32, :]).then_inc(s.st, 16)
+    g.wait_ge(s.lsem, lsum)
+    g.wait_ge(s.st, 64)
+
+
+def _relay(g, core, r, l, T, topo, P):
+    s = T.sem
+    cores, owners = P["cores"], P["owners"]
+    H = topo.host(core)
+    D = P["served"](H, l)
+    v, sc, pe = g.vector, g.scalar, g.tensor
+    hown = len(_engines(topo.mask(cores[r], core))) // LANES
+    lsum = 0
+
+    g.wait_ge(s.hown, hown)
+    me = TOK * D.index(r)
+    for call in P["hplan"](r, l):
+        trs = []
+        for (p, es) in call:
+            a = TOK * P["served"](topo.host(cores[p]), l).index(r)
+            trs.append(_tr(topo, core, owners[p][l], es, s.hpeer, T.Hd[:, me:me + TOK], T.Hd[:, a:a + TOK]))
+            lsum += len(es)
+        g.remote_dma_fused(trs, local_sem=s.lsem)
+
+    pe.wait_ge(s.hown, hown)
+    pe.wait_ge(s.hpeer, sum(P["count"](P["hplan"], p, l, r) for p in D if p != r))
+    n_on = len([e for e in _engines(topo.mask(cores[r], core))
+                if e not in _engines(topo.mask(cores[r], owners[P["twin"](r, P["fold"](H, l))][l]))]) // 2
+    src_far = cores[P["twin"](r, P["fold"](H, l))]
+    n_off = len(_engines(topo.mask(src_far, core))) // 2
+    pe.wait_ge(s.sowns, n_on)
+    for x in range(2):
+        pe.matmul((T.ps0 if x == 0 else T.ps1)[:, 0:SERVED * TOK], T.sown[:, BW * x:BW * x + BW], T.Hd[:], start=True, stop=False)
+    pe.wait_ge(s.sfars, n_off)
+    for x in range(2):
+        pe.matmul((T.ps0 if x == 0 else T.ps1)[:, 0:SERVED * TOK], T.sfar[:, BW * x:BW * x + BW], T.Hd[:], start=False,
+                  stop=True).then_inc(s.mm0 if x == 0 else s.mm1, 1)
+    v.wait_ge(s.mm0, 1)
+    v.tensor_copy(out=T.osb[:, :, 0, :], in_=T.ps0[:, 0:SERVED * TOK]).then_inc(s.cp, 1)
+    sc.wait_ge(s.mm1, 1)
+    sc.activation(out=T.osb[:, :, 1, :], in_=T.ps1[:, 0:SERVED * TOK], func=ActivationFunctionType.Copy).then_inc(s.cp, 1)
+
+    g.wait_ge(s.cp, 2)
+    for call in P["yplan"](r, l):
+        trs = []
+        for (p, es) in call:
+            i = P["served"](topo.host(cores[p]), l).index(r)
+            a = (i * LANES + l) * 2 * TOK
+            trs.append(_tr(topo, core, cores[p], es, s["y%d_%d" % (i, l // 2)], T.osb[:, D.index(p), :, :],
+                           T.land[:, a:a + 2 * TOK]))
+            lsum += len(es)
+        g.remote_dma_fused(trs, local_sem=s.lsem)
+    g.wait_ge(s.lsem, lsum)
+
+
+def rank_program(g, core, T, topo):
+    P = _plan(T, topo)
+    r = T.rank_of(core)
+    if r is not None:
+        _rank(g, core, r, T, topo, P)
+    elif core in P["relay"]:
+        q, l = P["relay"][core]
+        _relay(g, core, q, l, T, topo, P)

@@ -10,11 +10,13 @@ SERVED = 6
 SCRATCH = {
     "win": ("sbuf", [128, PAD + R + PAD], "bfloat16"),
     "negs": ("sbuf", [128, NS // 16], "int32"),
-    "offi": ("sbuf", [128, NS // 16], "int32"),
+    "negf": ("sbuf", [128, NS // 16], "float32"),
+    "rep": ("sbuf", [128, 128], "float32"),
     "off": ("sbuf", [128, NS // 16], "uint16"),
     "hsb": ("sbuf", [128, TOK], "bfloat16"),
     "S": ("sbuf", [128, NS], "bfloat16"),
     "ident": ("sbuf", [128, 128], "bfloat16"),
+    "idq": ("sbuf", [128, 128 // LANES], "bfloat16"),
     "land": ("sbuf", [128, SERVED * LANES * 2 * TOK], "bfloat16"),
     "ysb": ("sbuf", [128, 256], "bfloat16"),
     "sown": ("sbuf", [128, LW], "bfloat16"),
@@ -23,9 +25,11 @@ SCRATCH = {
     "osb": ("sbuf", [128, SERVED, 2, TOK], "bfloat16"),
     "ps0": ("psum", [128, 512], "float32"),
     "ps1": ("psum", [128, 512], "float32"),
+    "psn": ("psum", [128, 512], "float32"),
 }
-SEMAPHORES = ["hld", "negld", "tabld", "vz", "of1", "of2", "gA", "gB", "idn", "hown", "hpeer", "sowns", "sfars",
-              "mm0", "mm1", "cp", "pd0", "pd1", "ycp", "st", "lsem"] + ["y%d_%d" % (i, L) for i in range(SERVED) for L in range(2)]
+SEMAPHORES = ["hld", "negld", "tabld", "vr", "vz", "rp", "of1", "rpm", "of2", "gA", "gB", "ids", "idn", "hown", "hpeer",
+              "sowns", "sfars", "mm0", "mm1", "cp", "pd0", "pd1", "ycp0", "ycp1", "st", "lsem"] \
+    + ["y%d_%d" % (i, L) for i in range(SERVED) for L in range(2)]
 
 _C = {}
 
@@ -63,13 +67,12 @@ def _plan(T, topo):
         c = cores[q]
         H = topo.host(c)
         reach = [cores[p] for G in (H, near[H], far[H]) for p in byhost[G]]
-        owners.append([w for w in range(NSIM) if w != c and topo.host(w) == H and topo.chip(w) == topo.chip(c)
-                       and all(topo.may_write(w, d) for d in reach)][:LANES])
-    kind, seen = [], {}
-    for w in owners[0]:
-        k = seen.get(topo.die(w), 0)
-        kind.append(k % 2)
-        seen[topo.die(w)] = k + 1
+        cand = [w for w in range(NSIM) if w != c and topo.host(w) == H and topo.chip(w) == topo.chip(c)
+                and all(topo.may_write(w, d) for d in reach)]
+        same = [w for w in cand if topo.die(w) == topo.die(c)]
+        oth = [w for w in cand if topo.die(w) != topo.die(c)]
+        owners.append([same[0], oth[0], same[1], oth[1]])
+    kind = [(l % 2 + l // 2) % 2 for l in range(LANES)]
 
     def fold(H, l):
         return near[H] if kind[l] == 0 else far[H]
@@ -82,8 +85,11 @@ def _plan(T, topo):
 
     def targets(q, l):
         H = topo.host(cores[q])
-        D = served(H, l)
-        return [p for p in D if topo.host(cores[p]) != H] + [p for p in D if topo.host(cores[p]) == H and p != q]
+        X = serve(H, l)
+        oth = byhost[X] + [p for p in byhost[H] if p != q]
+        par = [p for p in byhost[H] if p != q and topo.may_write(cores[q], cores[p])] \
+            + [p for p in byhost[X] if topo.may_write(cores[q], cores[p])]
+        return [p for p in oth if p != par[0]] + [par[0]]
 
     def off_engines(q, l):
         m = topo.mask(owners[q][l], cores[q])
@@ -91,21 +97,26 @@ def _plan(T, topo):
             m &= topo.mask(owners[q][l], cores[p]) & topo.mask(owners[q][l], owners[p][l])
         return _engines(m)
 
+    def chip_engines(q, l):
+        es = off_engines(q, l)
+        return [e for e in _engines(topo.mask(owners[q][l], cores[q])) if e not in es]
+
     def hplan(q, l):
-        t, es = targets(q, l), off_engines(q, l)
+        tw = twin(q, serve(topo.host(cores[q]), l))
+        t, es = [p for p in targets(q, l) if p != tw], off_engines(q, l)
         k = len(es) // 4
-        return [[(t[j], es[k * j:k * j + k]) for j in range(4)], [(t[4], es)]]
+        return [[(t[j], es[k * j:k * j + k]) for j in range(4)]]
 
     def yplan(q, l):
         t, es = targets(q, l), off_engines(q, l)
-        k, h = len(es) // 4, len(es) // 2
-        return [[(t[j], es[k * j:k * j + k]) for j in range(4)], [(t[4], es[:h]), (q, es[h:])]]
+        k = len(es) // 4
+        return [[(t[j], es[k * j:k * j + k]) for j in range(4)] + [(q, chip_engines(q, l))], [(t[4], es)]]
 
     def count(plan, src, l, dst):
         return sum(len(e) for call in plan(src, l) for (p, e) in call if p == dst)
 
-    P = {"cores": cores, "owners": owners, "twin": twin, "fold": fold, "served": served, "hplan": hplan, "yplan": yplan,
-         "count": count, "relay": {owners[q][l]: (q, l) for q in range(n) for l in range(LANES)}}
+    P = {"cores": cores, "owners": owners, "twin": twin, "fold": fold, "serve": serve, "served": served, "hplan": hplan,
+         "yplan": yplan, "count": count, "relay": {owners[q][l]: (q, l) for q in range(n) for l in range(LANES)}}
     _C["p"] = P
     return P
 
@@ -115,84 +126,106 @@ def _tr(topo, src_core, dst_core, es, sem, src, dst):
     return RemoteDMATransfer(dst_ids=[DstId(rid=rid, pnc=pid)], dma_engine_mask=_bits(es), remote_sem=sem, src=src, dst=dst)
 
 
+def _rank_engines(topo, P, r):
+    c = P["cores"][r]
+    offc = _engines(topo.mask(c, P["owners"][P["twin"](r, P["fold"](topo.host(c), 0))][0]))
+    return offc, [e for e in _engines(topo.mask(c, P["owners"][r][0])) if e not in offc]
+
+
 def _rank(g, core, r, T, topo, P):
     s = T.sem
-    cores, owners = P["cores"], P["owners"]
+    owners = P["owners"]
     H = topo.host(core)
     v, sc, sy, pe = g.vector, g.scalar, g.sync, g.tensor
+    offc, onl = _rank_engines(topo, P, r)
+    lsum = 0
 
-    sy.dma_start(T.hsb[:], T.h[:]).then_inc(s.hld, 16)
-    for q in range(8):
-        (sy if q < 4 else sc).dma_start(T.negs[16 * q:16 * q + 16, :], T.neg[:]).then_inc(s.negld, 16)
+    sy.dma_start(T.negs[0:16, :], T.neg[:]).then_inc(s.negld, 16)
+    sc.dma_start(T.hsb[:], T.h[:]).then_inc(s.hld, 16)
     sy.dma_start(T.win[0:64, PAD:PAD + R], T.tab[0:64, :]).then_inc(s.tabld, 16)
     sc.dma_start(T.win[64:128, PAD:PAD + R], T.tab[64:128, :]).then_inc(s.tabld, 16)
 
+    v.memset(T.rep[0:16, :], 1.0).then_inc(s.vr, 1)
     v.memset(T.win[:, 0:PAD], 0.0).then_inc(s.vz, 1)
     v.memset(T.win[:, PAD + R:PAD + R + PAD], 0.0).then_inc(s.vz, 1)
-    v.memset(T.ident[:], 1.0).then_inc(s.vz, 1)
-    v.wait_ge(s.negld, 128)
-    v.tensor_scalar(out=T.offi[:], in0=T.negs[:], scalar1=float(PAD - R * r), scalar2=0.0,
+    g.wait_ge(s.vr, 1)
+    g.affine_select(out=T.rep[0:16, :], in_=T.rep[0:16, :], pattern=[[0, 8], [-1, 16]], compare_op=AluOpType.is_equal,
+                    fill=0.0, base=0, channel_multiplier=1).then_inc(s.rp, 1)
+    v.wait_ge(s.negld, 16)
+    v.tensor_scalar(out=T.negf[0:16, :], in0=T.negs[0:16, :], scalar1=float(PAD - R * r), scalar2=0.0,
                     op0=AluOpType.add, op1=AluOpType.max).then_inc(s.of1, 1)
-    v.wait_ge(s.of1, 1)
-    v.tensor_scalar(out=T.off[:], in0=T.offi[:], scalar1=float(PAD + R), scalar2=None, op0=AluOpType.min).then_inc(s.of2, 1)
+    pe.wait_ge(s.of1, 1)
+    pe.wait_ge(s.rp, 1)
+    pe.matmul(T.psn[:, 0:NS // 16], T.rep[0:16, :], T.negf[0:16, :], start=True, stop=True).then_inc(s.rpm, 1)
+    v.wait_ge(s.rpm, 1)
+    v.tensor_scalar(out=T.off[:], in0=T.psn[:, 0:NS // 16], scalar1=float(PAD + R), scalar2=None,
+                    op0=AluOpType.min).then_inc(s.of2, 1)
 
     g.wait_ge(s.hld, 16)
-    on = _engines(topo.mask(core, owners[r][0]))
-    k = len(on) // LANES
-    g.remote_dma_fused([_tr(topo, core, owners[r][l], on[k * l:k * l + k], s.hown, T.hsb[:],
-                            T.Hd[:, TOK * P["served"](H, l).index(r):TOK * P["served"](H, l).index(r) + TOK])
-                        for l in range(LANES)], local_sem=s.lsem)
-    lsum = len(on)
-    g.wait_ge(s.vz, 3)
-    g.affine_select(out=T.ident[:], in_=T.ident[:], pattern=[[-1, 128]], compare_op=AluOpType.is_equal, fill=0.0,
-                    base=0, channel_multiplier=1).then_inc(s.idn, 1)
+    k = len(onl) // LANES
+    trs = []
+    for l in range(LANES):
+        a = TOK * P["served"](H, l).index(r)
+        trs.append(_tr(topo, core, owners[r][l], onl[k * l:k * l + k], s.hown, T.hsb[:], T.Hd[:, a:a + TOK]))
+        lsum += k
+    g.remote_dma_fused(trs, local_sem=s.lsem)
+    k = len(offc) // LANES
+    trs = []
+    for l in range(LANES):
+        X = P["serve"](H, l)
+        a = TOK * P["served"](X, l).index(r)
+        trs.append(_tr(topo, core, owners[P["twin"](r, X)][l], offc[k * l:k * l + k], s.hpeer, T.hsb[:], T.Hd[:, a:a + TOK]))
+        lsum += k
+    g.remote_dma_fused(trs, local_sem=s.lsem)
 
     for q in (v, sc):
         q.wait_ge(s.of2, 1)
-        q.wait_ge(s.vz, 3)
+        q.wait_ge(s.vz, 2)
         q.wait_ge(s.tabld, 32)
-    for l in range(LANES):
-        L, bh = l // 2, l % 2
-        for x in range(2):
-            m = 2 * (2 * bh + x) + L
-            out = T.S[:, (2 * l + x) * BW:(2 * l + x + 1) * BW]
-            src = T.win[:, 0:PAD + R + PAD].indirect(T.off[:, 8 * m:8 * m + 8])
-            if bh == 0:
+    for L in range(2):
+        for j in range(2):
+            l = 2 * L + j
+            out = T.S[:, l * LW:(l + 1) * LW]
+            src = T.win[:, 0:PAD + R + PAD].indirect(T.off[:, (LW // 16) * l:(LW // 16) * (l + 1)])
+            if j == 0:
                 v.tensor_copy(out=out, in_=src).then_inc(s.gA if L == 0 else s.gB, 1)
             else:
                 sc.activation(out=out, in_=src, func=ActivationFunctionType.Copy).then_inc(s.gA if L == 0 else s.gB, 1)
     for L in range(2):
-        g.wait_ge(s.gA if L == 0 else s.gB, 4)
+        g.wait_ge(s.gA if L == 0 else s.gB, 2)
         trs = []
-        for j, l in enumerate((2 * L, 2 * L + 1)):
+        for j in range(2):
+            l = 2 * L + j
             dfar = owners[P["twin"](r, P["fold"](H, l))][l]
-            offc = _engines(topo.mask(core, dfar))
-            onl = [e for e in on if e not in offc]
-            h1, h2 = len(onl) // 2, len(offc) // 2
             blk = T.S[:, l * LW:(l + 1) * LW]
-            trs.append(_tr(topo, core, owners[r][l], onl[h1 * j:h1 * j + h1], s.sowns, blk, T.sown[:]))
-            trs.append(_tr(topo, core, dfar, offc[h2 * j:h2 * j + h2], s.sfars, blk, T.sfar[:]))
-            lsum += h1 + h2
+            e_on, e_off = onl[(j + L) % 2::2], offc[j::2]
+            trs.append(_tr(topo, core, owners[r][l], e_on, s.sowns, blk, T.sown[:]))
+            trs.append(_tr(topo, core, dfar, e_off, s.sfars, blk, T.sfar[:]))
+            lsum += len(e_on) + len(e_off)
         g.remote_dma_fused(trs, local_sem=s.lsem)
 
-    pe.wait_ge(s.idn, 1)
+    pe.wait_ge(s.idn, sum(len(_engines(topo.mask(owners[r][l], core))) for l in range(LANES)))
     for L in range(2):
         ps = T.ps0 if L == 0 else T.ps1
-        for i in range(SERVED):
+        late = [any(p == r for l in (2 * L, 2 * L + 1) for (p, e) in P["yplan"](P["served"](H, l)[i], l)[1])
+                for i in range(SERVED)]
+        order = [i for i in range(SERVED) if not late[i]] + [i for i in range(SERVED) if late[i]]
+        for o, i in enumerate(order):
             cnt = sum(P["count"](P["yplan"], P["served"](H, l)[i], l, r) for l in (2 * L, 2 * L + 1))
             pe.wait_ge(s["y%d_%d" % (i, L)], cnt)
             a = (i * LANES + 2 * L) * 2 * TOK
-            mm = pe.matmul(ps[:, 0:128], T.land[:, a:a + 128], T.ident[:], start=(i == 0), stop=(i == SERVED - 1))
+            mm = pe.matmul(ps[:, 0:128], T.land[:, a:a + 128], T.ident[:], start=(o == 0), stop=(o == SERVED - 1))
         mm.then_inc(s.pd0 if L == 0 else s.pd1, 1)
         v.wait_ge(s.pd0 if L == 0 else s.pd1, 1)
-        v.tensor_copy(out=T.ysb[:, 128 * L:128 * L + 128], in_=ps[:, 0:128]).then_inc(s.ycp, 1)
-    for b in range(4):
-        q = sy if b < 2 else sc
-        if b % 2 == 0:
-            q.wait_ge(s.ycp, 2)
-        q.dma_start(T.y[:, 256 * b:256 * b + 256], T.ysb[32 * b:32 * b + 32, :]).then_inc(s.st, 16)
+        v.tensor_copy(out=T.ysb[:, 128 * L:128 * L + 128], in_=ps[:, 0:128]).then_inc(s.ycp0 if L == 0 else s.ycp1, 1)
+        for b in range(4):
+            q = sy if b < 2 else sc
+            if b % 2 == 0:
+                q.wait_ge(s.ycp0 if L == 0 else s.ycp1, 1)
+            m = 4 * L + b
+            q.dma_start(T.y[:, BW * m:BW * m + BW], T.ysb[32 * b:32 * b + 32, 128 * L:128 * L + 128]).then_inc(s.st, 16)
     g.wait_ge(s.lsem, lsum)
-    g.wait_ge(s.st, 64)
+    g.wait_ge(s.st, 128)
 
 
 def _relay(g, core, r, l, T, topo, P):
@@ -201,9 +234,20 @@ def _relay(g, core, r, l, T, topo, P):
     H = topo.host(core)
     D = P["served"](H, l)
     v, sc, pe = g.vector, g.scalar, g.tensor
-    hown = len(_engines(topo.mask(cores[r], core))) // LANES
+    offc, onl = _rank_engines(topo, P, r)
     lsum = 0
 
+    w = 128 // LANES
+    v.memset(T.idq[:], 1.0).then_inc(s.vz, 1)
+    g.wait_ge(s.vz, 1)
+    g.affine_select(out=T.idq[:], in_=T.idq[:], pattern=[[-1, w]], compare_op=AluOpType.is_equal, fill=0.0,
+                    base=-w * l, channel_multiplier=1).then_inc(s.ids, 1)
+    g.wait_ge(s.ids, 1)
+    es = _engines(topo.mask(core, cores[r]))
+    g.remote_dma_fused([_tr(topo, core, cores[r], es, s.idn, T.idq[:], T.ident[:, w * l:w * l + w])], local_sem=s.lsem)
+    lsum += len(es)
+
+    hown = len(onl) // LANES
     g.wait_ge(s.hown, hown)
     me = TOK * D.index(r)
     for call in P["hplan"](r, l):
@@ -215,15 +259,11 @@ def _relay(g, core, r, l, T, topo, P):
         g.remote_dma_fused(trs, local_sem=s.lsem)
 
     pe.wait_ge(s.hown, hown)
-    pe.wait_ge(s.hpeer, sum(P["count"](P["hplan"], p, l, r) for p in D if p != r))
-    n_on = len([e for e in _engines(topo.mask(cores[r], core))
-                if e not in _engines(topo.mask(cores[r], owners[P["twin"](r, P["fold"](H, l))][l]))]) // 2
-    src_far = cores[P["twin"](r, P["fold"](H, l))]
-    n_off = len(_engines(topo.mask(src_far, core))) // 2
-    pe.wait_ge(s.sowns, n_on)
+    pe.wait_ge(s.hpeer, len(offc) // LANES + sum(P["count"](P["hplan"], p, l, r) for p in D if p != r))
+    pe.wait_ge(s.sowns, len(onl) // 2)
     for x in range(2):
         pe.matmul((T.ps0 if x == 0 else T.ps1)[:, 0:SERVED * TOK], T.sown[:, BW * x:BW * x + BW], T.Hd[:], start=True, stop=False)
-    pe.wait_ge(s.sfars, n_off)
+    pe.wait_ge(s.sfars, len(offc) // 2)
     for x in range(2):
         pe.matmul((T.ps0 if x == 0 else T.ps1)[:, 0:SERVED * TOK], T.sfar[:, BW * x:BW * x + BW], T.Hd[:], start=False,
                   stop=True).then_inc(s.mm0 if x == 0 else s.mm1, 1)

from concourse.bass import DstId, RemoteDMATransfer
from concourse.mybir import AluOpType, ActivationFunctionType

NSIM = 512
R, NS, TOK = 4096, 1024, 32
PAD = 8
LANES, LW, BW = 4, 256, 128
SERVED = 6

SCRATCH = {
    "win": ("sbuf", [128, PAD + R + PAD], "bfloat16"),
    "negs": ("sbuf", [128, NS // 16], "int32"),
    "negf": ("sbuf", [128, NS // 16], "float32"),
    "rep": ("sbuf", [128, 128], "float32"),
    "off": ("sbuf", [128, NS // 16], "uint16"),
    "hsb": ("sbuf", [128, TOK], "bfloat16"),
    "S": ("sbuf", [128, NS], "bfloat16"),
    "ident": ("sbuf", [128, 128], "bfloat16"),
    "idq": ("sbuf", [128, 128 // LANES], "bfloat16"),
    "land": ("sbuf", [128, SERVED * LANES * 2 * TOK], "bfloat16"),
    "ysb": ("sbuf", [128, 256], "bfloat16"),
    "sown": ("sbuf", [128, LW], "bfloat16"),
    "sfar": ("sbuf", [128, LW], "bfloat16"),
    "Hd": ("sbuf", [128, SERVED * TOK], "bfloat16"),
    "osb": ("sbuf", [128, SERVED, 2, TOK], "bfloat16"),
    "ps0": ("psum", [128, 512], "float32"),
    "ps1": ("psum", [128, 512], "float32"),
    "psn": ("psum", [128, 512], "float32"),
}
SEMAPHORES = ["hld", "negld", "tabld", "vr", "vz", "rp", "of1", "rpm", "of2", "gA", "gB", "ids", "idn", "hown", "hpeer",
              "sowns", "sfars", "mm0", "mm1", "cp", "pd0", "pd1", "ycp0", "ycp1", "st", "lsem"] \
    + ["y%d_%d" % (i, L) for i in range(SERVED) for L in range(2)]

_C = {}


def _engines(m):
    return [e for e in range(16) if (m >> e) & 1]


def _bits(es):
    return sum(1 << e for e in es)


def _plan(T, topo):
    if "p" in _C:
        return _C["p"]
    cores = list(T.cores)
    n = len(cores)
    hosts = sorted({topo.host(c) for c in cores})
    byhost = {H: [q for q in range(n) if topo.host(cores[q]) == H] for H in hosts}

    def twin(q, G):
        return [p for p in byhost[G] if topo.chip(cores[p]) == topo.chip(cores[q])][0]

    near, far = {}, {}
    for H in hosts:
        a = byhost[H][0]
        for G in hosts:
            if G != H and topo.may_write(cores[a], cores[twin(a, G)]):
                if topo.rack(G) == topo.rack(H):
                    near[H] = G
                else:
                    far[H] = G
    owners = []
    for q in range(n):
        c = cores[q]
        H = topo.host(c)
        reach = [cores[p] for G in (H, near[H], far[H]) for p in byhost[G]]
        cand = [w for w in range(NSIM) if w != c and topo.host(w) == H and topo.chip(w) == topo.chip(c)
                and all(topo.may_write(w, d) for d in reach)]
        same = [w for w in cand if topo.die(w) == topo.die(c)]
        oth = [w for w in cand if topo.die(w) != topo.die(c)]
        owners.append([same[0], oth[0], same[1], oth[1]])
    kind = [(l % 2 + l // 2) % 2 for l in range(LANES)]

    def fold(H, l):
        return near[H] if kind[l] == 0 else far[H]

    def serve(H, l):
        return far[H] if kind[l] == 0 else near[H]

    def served(H, l):
        return byhost[H] + byhost[serve(H, l)]

    def targets(q, l):
        H = topo.host(cores[q])
        X = serve(H, l)
        oth = byhost[X] + [p for p in byhost[H] if p != q]
        par = [p for p in byhost[H] if p != q and topo.may_write(cores[q], cores[p])] \
            + [p for p in byhost[X] if topo.may_write(cores[q], cores[p])]
        return [p for p in oth if p != par[0]] + [par[0]]

    def off_engines(q, l):
        m = topo.mask(owners[q][l], cores[q])
        for p in targets(q, l):
            m &= topo.mask(owners[q][l], cores[p]) & topo.mask(owners[q][l], owners[p][l])
        return _engines(m)

    def chip_engines(q, l):
        es = off_engines(q, l)
        return [e for e in _engines(topo.mask(owners[q][l], cores[q])) if e not in es]

    def hplan(q, l):
        tw = twin(q, serve(topo.host(cores[q]), l))
        t, es = [p for p in targets(q, l) if p != tw], off_engines(q, l)
        k = len(es) // 4
        return [[(t[j], es[k * j:k * j + k]) for j in range(4)]]

    def yplan(q, l):
        t, es = targets(q, l), off_engines(q, l)
        k = len(es) // 4
        return [[(t[j], es[k * j:k * j + k]) for j in range(4)] + [(q, chip_engines(q, l))], [(t[4], es)]]

    def count(plan, src, l, dst):
        return sum(len(e) for call in plan(src, l) for (p, e) in call if p == dst)

    P = {"cores": cores, "owners": owners, "twin": twin, "fold": fold, "serve": serve, "served": served, "hplan": hplan,
         "yplan": yplan, "count": count, "relay": {owners[q][l]: (q, l) for q in range(n) for l in range(LANES)}}
    _C["p"] = P
    return P


def _tr(topo, src_core, dst_core, es, sem, src, dst):
    rid, pid = topo.addr(dst_core, src_core)
    return RemoteDMATransfer(dst_ids=[DstId(rid=rid, pnc=pid)], dma_engine_mask=_bits(es), remote_sem=sem, src=src, dst=dst)


def _rank_engines(topo, P, r):
    c = P["cores"][r]
    offc = _engines(topo.mask(c, P["owners"][P["twin"](r, P["fold"](topo.host(c), 0))][0]))
    return offc, [e for e in _engines(topo.mask(c, P["owners"][r][0])) if e not in offc]


def _rank(g, core, r, T, topo, P):
    s = T.sem
    owners = P["owners"]
    H = topo.host(core)
    v, sc, sy, pe = g.vector, g.scalar, g.sync, g.tensor
    offc, onl = _rank_engines(topo, P, r)
    lsum = 0

    sy.dma_start(T.negs[0:16, :], T.neg[:]).then_inc(s.negld, 16)
    sc.dma_start(T.hsb[:], T.h[:]).then_inc(s.hld, 16)
    sy.dma_start(T.win[0:64, PAD:PAD + R], T.tab[0:64, :]).then_inc(s.tabld, 16)
    sc.dma_start(T.win[64:128, PAD:PAD + R], T.tab[64:128, :]).then_inc(s.tabld, 16)

    v.memset(T.rep[0:16, :], 1.0).then_inc(s.vr, 1)
    v.memset(T.win[:, 0:PAD], 0.0).then_inc(s.vz, 1)
    v.memset(T.win[:, PAD + R:PAD + R + PAD], 0.0).then_inc(s.vz, 1)
    g.wait_ge(s.vr, 1)
    g.affine_select(out=T.rep[0:16, :], in_=T.rep[0:16, :], pattern=[[0, 8], [-1, 16]], compare_op=AluOpType.is_equal,
                    fill=0.0, base=0, channel_multiplier=1).then_inc(s.rp, 1)
    v.wait_ge(s.negld, 16)
    v.tensor_scalar(out=T.negf[0:16, :], in0=T.negs[0:16, :], scalar1=float(PAD - R * r), scalar2=0.0,
                    op0=AluOpType.add, op1=AluOpType.max).then_inc(s.of1, 1)
    pe.wait_ge(s.of1, 1)
    pe.wait_ge(s.rp, 1)
    pe.matmul(T.psn[:, 0:NS // 16], T.rep[0:16, :], T.negf[0:16, :], start=True, stop=True).then_inc(s.rpm, 1)
    v.wait_ge(s.rpm, 1)
    v.tensor_scalar(out=T.off[:], in0=T.psn[:, 0:NS // 16], scalar1=float(PAD + R), scalar2=None,
                    op0=AluOpType.min).then_inc(s.of2, 1)

    g.wait_ge(s.hld, 16)
    k = len(onl) // LANES
    trs = []
    for l in range(LANES):
        a = TOK * P["served"](H, l).index(r)
        trs.append(_tr(topo, core, owners[r][l], onl[k * l:k * l + k], s.hown, T.hsb[:], T.Hd[:, a:a + TOK]))
        lsum += k
    g.remote_dma_fused(trs, local_sem=s.lsem)
    k = len(offc) // LANES
    trs = []
    for l in range(LANES):
        X = P["serve"](H, l)
        a = TOK * P["served"](X, l).index(r)
        trs.append(_tr(topo, core, owners[P["twin"](r, X)][l], offc[k * l:k * l + k], s.hpeer, T.hsb[:], T.Hd[:, a:a + TOK]))
        lsum += k
    g.remote_dma_fused(trs, local_sem=s.lsem)

    for q in (v, sc):
        q.wait_ge(s.of2, 1)
        q.wait_ge(s.vz, 2)
        q.wait_ge(s.tabld, 32)
    for L in range(2):
        for j in range(2):
            l = 2 * L + j
            out = T.S[:, l * LW:(l + 1) * LW]
            src = T.win[:, 0:PAD + R + PAD].indirect(T.off[:, (LW // 16) * l:(LW // 16) * (l + 1)])
            if j == 0:
                v.tensor_copy(out=out, in_=src).then_inc(s.gA if L == 0 else s.gB, 1)
            else:
                sc.activation(out=out, in_=src, func=ActivationFunctionType.Copy).then_inc(s.gA if L == 0 else s.gB, 1)
    for L in range(2):
        g.wait_ge(s.gA if L == 0 else s.gB, 2)
        trs = []
        for j in range(2):
            l = 2 * L + j
            dfar = owners[P["twin"](r, P["fold"](H, l))][l]
            blk = T.S[:, l * LW:(l + 1) * LW]
            e_on, e_off = onl[(j + L) % 2::2], offc[j::2]
            trs.append(_tr(topo, core, owners[r][l], e_on, s.sowns, blk, T.sown[:]))
            trs.append(_tr(topo, core, dfar, e_off, s.sfars, blk, T.sfar[:]))
            lsum += len(e_on) + len(e_off)
        g.remote_dma_fused(trs, local_sem=s.lsem)

    pe.wait_ge(s.idn, sum(len(_engines(topo.mask(owners[r][l], core))) for l in range(LANES)))
    for L in range(2):
        ps = T.ps0 if L == 0 else T.ps1
        late = [any(p == r for l in (2 * L, 2 * L + 1) for (p, e) in P["yplan"](P["served"](H, l)[i], l)[1])
                for i in range(SERVED)]
        order = [i for i in range(SERVED) if not late[i]] + [i for i in range(SERVED) if late[i]]
        for o, i in enumerate(order):
            cnt = sum(P["count"](P["yplan"], P["served"](H, l)[i], l, r) for l in (2 * L, 2 * L + 1))
            pe.wait_ge(s["y%d_%d" % (i, L)], cnt)
            a = (i * LANES + 2 * L) * 2 * TOK
            mm = pe.matmul(ps[:, 0:128], T.land[:, a:a + 128], T.ident[:], start=(o == 0), stop=(o == SERVED - 1))
        mm.then_inc(s.pd0 if L == 0 else s.pd1, 1)
        v.wait_ge(s.pd0 if L == 0 else s.pd1, 1)
        v.tensor_copy(out=T.ysb[:, 128 * L:128 * L + 128], in_=ps[:, 0:128]).then_inc(s.ycp0 if L == 0 else s.ycp1, 1)
        for b in range(4):
            q = sy if b < 2 else sc
            if b % 2 == 0:
                q.wait_ge(s.ycp0 if L == 0 else s.ycp1, 1)
            m = 4 * L + b
            q.dma_start(T.y[:, BW * m:BW * m + BW], T.ysb[32 * b:32 * b + 32, 128 * L:128 * L + 128]).then_inc(s.st, 16)
    g.wait_ge(s.lsem, lsum)
    g.wait_ge(s.st, 128)


def _relay(g, core, r, l, T, topo, P):
    s = T.sem
    cores, owners = P["cores"], P["owners"]
    H = topo.host(core)
    D = P["served"](H, l)
    v, sc, pe = g.vector, g.scalar, g.tensor
    offc, onl = _rank_engines(topo, P, r)
    lsum = 0

    w = 128 // LANES
    v.memset(T.idq[:], 1.0).then_inc(s.vz, 1)
    g.wait_ge(s.vz, 1)
    g.affine_select(out=T.idq[:], in_=T.idq[:], pattern=[[-1, w]], compare_op=AluOpType.is_equal, fill=0.0,
                    base=-w * l, channel_multiplier=1).then_inc(s.ids, 1)
    g.wait_ge(s.ids, 1)
    es = _engines(topo.mask(core, cores[r]))
    g.remote_dma_fused([_tr(topo, core, cores[r], es, s.idn, T.idq[:], T.ident[:, w * l:w * l + w])], local_sem=s.lsem)
    lsum += len(es)

    hown = len(onl) // LANES
    g.wait_ge(s.hown, hown)
    me = TOK * D.index(r)
    for call in P["hplan"](r, l):
        trs = []
        for (p, es) in call:
            a = TOK * P["served"](topo.host(cores[p]), l).index(r)
            trs.append(_tr(topo, core, owners[p][l], es, s.hpeer, T.Hd[:, me:me + TOK], T.Hd[:, a:a + TOK]))
            lsum += len(es)
        g.remote_dma_fused(trs, local_sem=s.lsem)

    pe.wait_ge(s.hown, hown)
    pe.wait_ge(s.hpeer, len(offc) // LANES + sum(P["count"](P["hplan"], p, l, r) for p in D if p != r))
    pe.wait_ge(s.sowns, len(onl) // 2)
    for x in range(2):
        pe.matmul((T.ps0 if x == 0 else T.ps1)[:, 0:SERVED * TOK], T.sown[:, BW * x:BW * x + BW], T.Hd[:], start=True, stop=False)
    pe.wait_ge(s.sfars, len(offc) // 2)
    for x in range(2):
        pe.matmul((T.ps0 if x == 0 else T.ps1)[:, 0:SERVED * TOK], T.sfar[:, BW * x:BW * x + BW], T.Hd[:], start=False,
                  stop=True).then_inc(s.mm0 if x == 0 else s.mm1, 1)
    v.wait_ge(s.mm0, 1)
    v.tensor_copy(out=T.osb[:, :, 0, :], in_=T.ps0[:, 0:SERVED * TOK]).then_inc(s.cp, 1)
    sc.wait_ge(s.mm1, 1)
    sc.activation(out=T.osb[:, :, 1, :], in_=T.ps1[:, 0:SERVED * TOK], func=ActivationFunctionType.Copy).then_inc(s.cp, 1)

    g.wait_ge(s.cp, 2)
    for call in P["yplan"](r, l):
        trs = []
        for (p, es) in call:
            i = P["served"](topo.host(cores[p]), l).index(r)
            a = (i * LANES + l) * 2 * TOK
            trs.append(_tr(topo, core, cores[p], es, s["y%d_%d" % (i, l // 2)], T.osb[:, D.index(p), :, :],
                           T.land[:, a:a + 2 * TOK]))
            lsum += len(es)
        g.remote_dma_fused(trs, local_sem=s.lsem)
    g.wait_ge(s.lsem, lsum)


def rank_program(g, core, T, topo):
    P = _plan(T, topo)
    r = T.rank_of(core)
    if r is not None:
        _rank(g, core, r, T, topo, P)
    elif core in P["relay"]:
        q, l = P["relay"][core]
        _relay(g, core, q, l, T, topo, P)
